import numpy as np
import ml_dtypes


def mxq(x, axis, fmt="e4m3"):
    dtype, down = {"e4m3": (ml_dtypes.float8_e4m3fn, 7), "e5m2": (ml_dtypes.float8_e5m2, 14)}[fmt]
    v = np.moveaxis(np.asarray(x, np.float32).astype(ml_dtypes.bfloat16).astype(np.float64), axis, -1)
    blocks = v.reshape(v.shape[:-1] + (-1, 32))
    amax = np.abs(blocks).max(-1, keepdims=True)
    byte = np.maximum(np.where(amax > 0, np.frexp(amax)[1] - 1 + 127, 0) - down, 1)
    scale = np.exp2(byte - 127.0)
    codes = (blocks / scale).astype(np.float32).astype(dtype).astype(np.float64)
    return np.moveaxis((codes * scale).reshape(v.shape), -1, axis)


WIDE = False


def mx_kscale(k):
    if not WIDE:
        return np.ones(k)
    levels = np.array([10, -10, 5, -5, 0])
    if k % 512:
        return np.exp2(np.random.permutation(np.resize(levels, k // 32))).repeat(32)
    a = np.empty((k // 512, 16))
    for p in range(k // 512):
        a[p, :8] = np.random.permutation(np.resize(levels, 8))
        for g in range(8):
            far = levels[np.abs(levels - a[p, g]) >= 10]
            a[p, g + 8] = far[np.random.randint(len(far))]
    return np.exp2(a.ravel()).repeat(32)


def f64(x):
    return np.asarray(x).astype(np.float64)


E2M1 = np.array([0.0, 0.5, 1.0, 1.5, 2.0, 3.0, 4.0, 6.0, -0.0, -0.5, -1.0, -1.5, -2.0, -3.0, -4.0, -6.0])


def pack_weight(w, fmt):
    k, n = w.shape
    w = f64(np.asarray(w, np.float32).astype(ml_dtypes.bfloat16)).reshape(k // 32, 32, n)
    amax = np.abs(w).max(1)
    if fmt == "e4m3":
        byte = np.frexp(amax)[1] - 1 + 127 - 7
    else:
        mant, ex = np.frexp(amax / 6.0)
        byte = np.where(mant > 0.5, ex, ex - 1) + 127
    byte = np.clip(np.where(amax > 0, byte, 1), 1, 254)
    scaled = (w * np.exp2(127.0 - byte)[:, None, :]).reshape(k, n).astype(np.float32)
    by_word = np.ascontiguousarray(scaled.reshape(k // 512, 128, 4, n).transpose(0, 1, 3, 2))
    if fmt == "e4m3":
        words = by_word.astype(ml_dtypes.float8_e4m3fn).view(np.uint8)
    else:
        c = by_word.astype(ml_dtypes.float4_e2m1fn).view(np.uint8) & 0xF
        words = (c[..., 0::2] | (c[..., 1::2] << 4)).reshape(k // 512, 128, 2 * n)
    return np.ascontiguousarray(words), np.ascontiguousarray(byte.astype(np.uint8).reshape(k // 512, 16, n))


def unpack_weight(words, scales, fmt):
    g, _, n = scales.shape
    words = np.ascontiguousarray(words).reshape(g, 128, n, -1)
    if fmt == "e4m3":
        vals = words.view(ml_dtypes.float8_e4m3fn).astype(np.float64)
    else:
        nib = np.empty((g, 128, n, 4), np.uint8)
        nib[..., 0::2] = words & 0xF
        nib[..., 1::2] = words >> 4
        vals = E2M1[nib]
    vals = vals * np.repeat(np.exp2(scales.astype(np.float64) - 127.0), 8, axis=1)[..., None]
    return vals.transpose(0, 1, 3, 2).reshape(g * 512, n)


def planes(y):
    n, m = y.shape
    v = y.astype(np.float32).astype(ml_dtypes.bfloat16).astype(np.float64).reshape(n // 32, 32, m)
    top = np.abs(v).max(1)
    byte = np.clip(np.where(top > 0, np.frexp(top)[1] - 1 + 127 - 7, 1), 1, 254)
    codes = (v * np.exp2(127.0 - byte)[:, None, :]).reshape(n, m).astype(np.float32).astype(ml_dtypes.float8_e4m3fn).view(np.uint8)
    words = codes.reshape(n // 512, 128, 4, m).transpose(0, 1, 3, 2)
    return np.ascontiguousarray(words), np.ascontiguousarray(byte.astype(np.uint8).reshape(n // 512, 16, m))


O, K, R, M, T = 1024, 2560, 512, 1024, 512


def setup_inputs():
    n = np.random.standard_normal
    s = mx_kscale(K)[:, None]
    u = mx_kscale(R)[:, None]
    x = n((K, T)); x[:O] *= 6.0
    w = n((K, M)) / np.sqrt(K) / s; w[:O] /= 2.0
    p_w8 = pack_weight(w[:O], "e4m3")
    p_w4 = pack_weight(w[O:], "e2m1")
    p_up = pack_weight(n((R, M)) / np.sqrt(R) / u, "e2m1")
    return {
        "x": (x * s).astype(np.float32),
        "w8_words": p_w8[0],
        "w8_scales": p_w8[1],
        "w4_words": p_w4[0],
        "w4_scales": p_w4[1],
        "down": (0.3 * n((K, R)) / np.sqrt(K) / s * u.T).astype(np.float32),
        "up_words": p_up[0],
        "up_scales": p_up[1],
        "g": (n((512, 1024))).astype(np.float32),
    }


def reference(x, w8_words, w8_scales, w4_words, w4_scales, down, up_words, up_scales, g):
    x_ = mxq(f64(x), 0, "e4m3")
    w8_ = unpack_weight(w8_words, w8_scales, "e4m3")
    w4_ = unpack_weight(w4_words, w4_scales, "e2m1")
    down_ = mxq(f64(down), 0, "e4m3")
    up_ = unpack_weight(up_words, up_scales, "e2m1")
    h_ = mxq(down_.T @ x_, 0, "e4m3")
    y = x_[:O].T @ w8_ + x_[O:].T @ w4_ + h_.T @ up_
    out_0 = f64(g) * y
    return (out_0,) + planes(out_0)

@@ -1,0 +1,266 @@
+from contextlib import ExitStack
+
+import concourse.mybir as mybir
+
+O, K, R, M, T = 1024, 2560, 512, 1024, 512
+FLOPS = 2 * (K * R * T + K * T * M + R * T * M)
+
+F32 = mybir.dt.float32
+BF16 = mybir.dt.bfloat16
+I32 = mybir.dt.int32
+U32 = mybir.dt.uint32
+U8 = mybir.dt.uint8
+FP8X4 = mybir.dt.float8_e4m3fn_x4
+FP4X4 = mybir.dt.float4_e2m1fn_x4
+MULT = mybir.AluOpType.mult
+
+P = 128
+PACK = 4
+K_PASS = P * PACK
+HALF = M // 2
+W8_PASSES = O // K_PASS
+W4_PASSES = (K - O) // K_PASS
+QUADS = 4
+W8_ROW = 4
+
+
+def tile_mix_three_tm_pl_mul_kernel(
+    tc, x, w8_words, w8_scales, w4_words, w4_scales, down, up_words, up_scales, g, out_0, out_1, out_2
+):
+    nc = tc.nc
+    with ExitStack() as ctx:
+        sb = ctx.enter_context(tc.tile_pool(name="sb", bufs=1))
+        ps = ctx.enter_context(tc.psum_pool(name="ps", bufs=1))
+        ctx.enter_context(tc.manual_schedule())
+
+        def new(name, shape, dtype):
+            return sb.tile(shape, dtype, name=name, align_bytes=64)
+
+        def load_rows(name, src, a, c0, c1):
+            raw = new(name, [P, PACK, c1 - c0], F32)
+            rows = src[a * K_PASS : (a + 1) * K_PASS, :].rearrange("(p j) c -> p j c", j=PACK)
+            nc.sync.dma_start(out=raw[:], in_=rows[:, :, c0:c1])
+            return raw
+
+        def load_w8(a, half):
+            words = new("w8_%d_%d" % (a, half), [P, HALF], U32)
+            src = w8_words[a].rearrange("p n i -> p (n i)")[:, half * 4 * HALF : (half + 1) * 4 * HALF]
+            nc.sync.dma_start(out=words[:].bitcast(I32), in_=src.bitcast(I32))
+            return words
+
+        def load_fp4(name, src_words, half):
+            passes = src_words.shape[0]
+            words = new("%s_%d" % (name, half), [P, passes, 2 * HALF], U8)
+            src = src_words.rearrange("a p c -> p a c")[:, :, half * 2 * HALF : (half + 1) * 2 * HALF]
+            nc.sync.dma_start(out=words[:].bitcast(I32), in_=src.bitcast(I32))
+            return words
+
+        g_rows = g.rearrange("(p i) n -> p i n", i=PACK)
+        out_rows = out_0.rearrange("(p i) n -> p i n", i=PACK)
+        out_words = out_1[0].rearrange("p n i -> p (n i)")
+
+        w4_sc = new("w4_sc", [P, W4_PASSES, M], U8)
+        w8_sc = new("w8_sc", [P, M], U8)
+        up_sc = new("up_sc", [P, M], U8)
+        for plane in (w4_sc, w8_sc, up_sc):
+            nc.vector.memset(plane[:].bitcast(I32), 0)
+        for q in range(QUADS):
+            nc.gpsimd.dma_start(
+                out=w4_sc[32 * q : 32 * q + 4, :, :].bitcast(I32),
+                in_=w4_scales[:, 4 * q : 4 * q + 4, :].rearrange("a r n -> r a n").bitcast(I32),
+            )
+        for q in range(QUADS):
+            nc.gpsimd.dma_start(
+                out=w8_sc[32 * q + W8_ROW : 32 * q + W8_ROW + 4 * W8_PASSES, :].bitcast(I32),
+                in_=w8_scales[:, 4 * q : 4 * q + 4, :].bitcast(I32),
+            )
+        for q in range(QUADS):
+            nc.gpsimd.dma_start(
+                out=up_sc[32 * q : 32 * q + 4, :].bitcast(I32),
+                in_=up_scales[0, 4 * q : 4 * q + 4, :].bitcast(I32),
+            )
+
+        order = [2, 3, 4, 0, 1]
+        last = order[-1]
+        x_raw, d_raw, w8, w4, up = {}, {}, {}, {}, {}
+        for a in order[:-1]:
+            d_raw[a] = load_rows("d_raw%d" % a, down, a, 0, R)
+            x_raw[a] = load_rows("x_raw%d" % a, x, a, 0, T)
+            if a == 4:
+                w4[0] = load_fp4("w4", w4_words, 0)
+        w8[0, 0] = load_w8(0, 0)
+        d_raw[last] = load_rows("d_raw%d" % last, down, last, 0, R)
+        x_last = [load_rows("x_last%d" % u, x, last, u * T // 2, (u + 1) * T // 2) for u in range(2)]
+        w8[1, 0] = load_w8(1, 0)
+        up[0] = load_fp4("up", up_words, 0)
+        w4[1] = load_fp4("w4", w4_words, 1)
+        w8[0, 1] = load_w8(0, 1)
+        w8[1, 1] = load_w8(1, 1)
+        g0 = []
+        for i in range(PACK):
+            g0.append(new("g0_%d" % i, [P, HALF], F32))
+            nc.sync.dma_start(out=g0[i][:], in_=g_rows[:, i, 0:HALF])
+            if i == 1:
+                up[1] = load_fp4("up", up_words, 1)
+        g1 = new("g1", [P, PACK, HALF], F32)
+        nc.sync.dma_start(out=g1[:], in_=g_rows[:, :, HALF:M])
+
+        def deal(dealt, halves):
+            dst = dealt[:].rearrange("p i m j -> p m i j")
+            for u, copy in ((0, nc.scalar.copy), (1, nc.vector.tensor_copy)):
+                copy(out=dst[:, 64 * u : 64 * (u + 1), :, :], in_=halves[u].rearrange("p j (m i) -> p m i j", i=PACK))
+
+        def quantize(codes, scales, values):
+            nc.vector.quantize_mx(out=codes.bitcast(FP8X4), scales=scales, in_=values)
+
+        def prepare(name, halves, pieces):
+            dealt = new(name + "_bf", [P, PACK, P, PACK], BF16)
+            codes = new(name + "_codes", [P, PACK * P], U32)
+            scales = new(name + "_scales", [P, PACK * P], U8)
+            deal(dealt, halves)
+            flat = dealt[:].rearrange("p i m j -> p (i m j)")
+            width = PACK * P // pieces
+            for c in range(pieces):
+                cols = slice(c * width, (c + 1) * width)
+                quantize(codes[:, cols], scales[:, cols], flat[:, PACK * c * width : PACK * (c + 1) * width])
+            return codes, scales
+
+        def split(raw):
+            return [raw[:, :, 0:256], raw[:, :, 256:512]]
+
+        h_ps = [ps.tile([P, PACK, P], F32, name="h_ps%d" % i, tag="bank%d" % i) for i in range(PACK)]
+        y0_ps = [ps.tile([P, HALF], F32, name="y0_ps%d" % i, tag="bank%d" % (PACK + i)) for i in range(PACK)]
+        xq, dq, hq = {}, {}, {}
+
+        def block(i):
+            return slice(i * P, (i + 1) * P)
+
+        def h_pass(a, i):
+            for j in range(PACK):
+                nc.tensor.matmul_mx(
+                    out=h_ps[i][:, j, :],
+                    lhsT=dq[a][0][:, block(j)].bitcast(FP8X4),
+                    lhsT_scale=dq[a][1][:, block(j)],
+                    rhs=xq[a][0][:, block(i)].bitcast(FP8X4),
+                    rhs_scale=xq[a][1][:, block(i)],
+                    start=(a == order[0] and j == 0),
+                    stop=(a == last and j == PACK - 1),
+                )
+
+        UP = "up"
+
+        def y_pass(out, a, i, n0, width, start, stop):
+            half, c0 = divmod(n0, HALF)
+            if a == UP:
+                lhs, lhs_sc = hq[i][0][:], hq[i][1][:]
+                rhs = up[half][:, 0, 2 * c0 : 2 * (c0 + width)].bitcast(FP4X4)
+                rhs_sc = up_sc[:, n0 : n0 + width]
+            else:
+                lhs, lhs_sc = xq[a][0][:, block(i)], xq[a][1][:, block(i)]
+                if a < W8_PASSES:
+                    rhs = w8[a, half][:, c0 : c0 + width].bitcast(FP8X4)
+                    rhs_sc = w8_sc[W8_ROW + 4 * a : P, n0 : n0 + width]
+                else:
+                    rhs = w4[half][:, a - W8_PASSES, 2 * c0 : 2 * (c0 + width)].bitcast(FP4X4)
+                    rhs_sc = w4_sc[:, a - W8_PASSES, n0 : n0 + width]
+            nc.tensor.matmul_mx(
+                out=out, lhsT=lhs.bitcast(FP8X4), lhsT_scale=lhs_sc, rhs=rhs, rhs_scale=rhs_sc, start=start, stop=stop
+            )
+
+        def y0_pass(a):
+            for i in range(PACK):
+                y_pass(y0_ps[i][:], a, i, 0, HALF, a == order[0], a == UP)
+
+        for a in order[:-1]:
+            dq[a] = prepare("d%d" % a, split(d_raw[a]), 1)
+            xq[a] = prepare("x%d" % a, split(x_raw[a]), 1)
+            for i in range(PACK):
+                h_pass(a, i)
+            if a == 4:
+                for b in order[:3]:
+                    y0_pass(b)
+        y0_pass(0)
+        dq[last] = prepare("d%d" % last, split(d_raw[last]), 1)
+        xq[last] = prepare("x%d" % last, [half[:] for half in x_last], PACK)
+        for i in range(PACK):
+            h_pass(last, i)
+        y0_pass(last)
+
+        h_bf = [new("h_bf%d" % i, [P, P, PACK], BF16) for i in range(PACK)]
+        for i in range(PACK):
+            hq[i] = (new("h_codes%d" % i, [P, P], U32), new("h_scales%d" % i, [P, P], U8))
+
+        def h_out(i, copy):
+            copy(out=h_bf[i][:], in_=h_ps[i][:].rearrange("p j t -> p t j"))
+
+        def h_quant(i):
+            quantize(hq[i][0][:], hq[i][1][:], h_bf[i][:].rearrange("p t j -> p (t j)"))
+
+        h_out(0, nc.scalar.copy)
+        h_out(1, nc.vector.tensor_copy)
+        h_out(2, nc.scalar.copy)
+        h_quant(0)
+        h_quant(1)
+        h_out(3, nc.vector.tensor_copy)
+        h_quant(2)
+        h_quant(3)
+        y0_pass(UP)
+
+        y1_ps = []
+        for c in range(PACK):
+            y1_ps.append(ps.tile([P, PACK, P], F32, name="y1_ps%d" % c, tag="bank%d" % c))
+            for i in range(PACK):
+                for a in order + [UP]:
+                    y_pass(y1_ps[c][:, i, :], a, i, HALF + c * P, P, a == order[0], a == UP)
+
+        o_words = new("o_words", [P, M], U32)
+        o_scales = new("o_scales", [P, M], U8)
+
+        def interleave(name, res, c0, width, copy):
+            o_bf = new(name, [P, width, PACK], BF16)
+            copy(out=o_bf[:], in_=res[:, :, c0 : c0 + width].rearrange("p i n -> p n i"))
+            return o_bf
+
+        def o_quant(o_bf, n0):
+            cols = slice(n0, n0 + o_bf.shape[1])
+            quantize(o_words[:, cols], o_scales[:, cols], o_bf[:].rearrange("p n i -> p (n i)"))
+
+        def store_words(n0, n1):
+            nc.sync.dma_start(out=out_words[:, 4 * n0 : 4 * n1].bitcast(I32), in_=o_words[:, n0:n1].bitcast(I32))
+
+        def mul1(res, c0, c):
+            nc.vector.tensor_tensor(out=res[:, :, c0 : c0 + P], in0=y1_ps[c][:], in1=g1[:, :, block(c)], op=MULT)
+
+        res0 = new("res0", [P, PACK, HALF], F32)
+        for i in range(PACK):
+            nc.vector.tensor_tensor(out=res0[:, i, :], in0=y0_ps[i][:], in1=g0[i][:], op=MULT)
+            nc.sync.dma_start(out=out_rows[:, i, 0:HALF], in_=res0[:, i, :])
+        res1a = new("res1a", [P, PACK, 2 * P], F32)
+        res1b = new("res1b", [P, PACK, P], F32)
+        res1c = new("res1c", [P, PACK, P], F32)
+
+        bf0b = interleave("bf0b", res0, 256, 256, nc.scalar.copy)
+        mul1(res1a, 0, 0)
+        bf0a = interleave("bf0a", res0, 0, 256, nc.vector.tensor_copy)
+        mul1(res1a, P, 1)
+        nc.sync.dma_start(out=out_rows[:, :, HALF : HALF + 2 * P], in_=res1a[:])
+        bf1a = interleave("bf1a", res1a, 0, 256, nc.scalar.copy)
+        o_quant(bf0a, 0)
+        o_quant(bf0b, 256)
+        store_words(0, HALF)
+        mul1(res1b, 0, 2)
+        nc.sync.dma_start(out=out_rows[:, :, HALF + 2 * P : HALF + 3 * P], in_=res1b[:])
+        bf1b = interleave("bf1b", res1b, 0, P, nc.scalar.copy)
+        o_quant(bf1a, HALF)
+        o_quant(bf1b, HALF + 2 * P)
+        store_words(HALF, HALF + 3 * P)
+        mul1(res1c, 0, 3)
+        nc.sync.dma_start(out=out_rows[:, :, HALF + 3 * P : M], in_=res1c[:])
+        bf1c = interleave("bf1c", res1c, 0, P, nc.vector.tensor_copy)
+        o_quant(bf1c, HALF + 3 * P)
+        store_words(HALF + 3 * P, M)
+        for q in range(QUADS):
+            queue = nc.scalar if q % 2 == 0 else nc.sync
+            queue.dma_start(
+                out=out_2[0, 4 * q : 4 * q + 4, :].bitcast(I32), in_=o_scales[32 * q : 32 * q + 4, :].bitcast(I32)
+            )

@@ -22,6 +22,7 @@ W8_PASSES = O // K_PASS
 W4_PASSES = (K - O) // K_PASS
 QUADS = 4
 W8_ROW = 4
+SCALAR_SHARE = 56
 
 
 def tile_mix_three_tm_pl_mul_kernel(
@@ -48,12 +49,11 @@ def tile_mix_three_tm_pl_mul_kernel(
             nc.sync.dma_start(out=words[:].bitcast(I32), in_=src.bitcast(I32))
             return words
 
-        def load_fp4(name, src_words, half):
-            passes = src_words.shape[0]
-            words = new("%s_%d" % (name, half), [P, passes, 2 * HALF], U8)
-            src = src_words.rearrange("a p c -> p a c")[:, :, half * 2 * HALF : (half + 1) * 2 * HALF]
+        def load_fp4(name, src_words, a0, a1, n0, n1):
+            words = new(name, [P, a1 - a0, 2 * (n1 - n0)], U8)
+            src = src_words.rearrange("a p c -> p a c")[:, a0:a1, 2 * n0 : 2 * n1]
             nc.sync.dma_start(out=words[:].bitcast(I32), in_=src.bitcast(I32))
-            return words
+            return [words[:, a, :] for a in range(a1 - a0)]
 
         g_rows = g.rearrange("(p i) n -> p i n", i=PACK)
         out_rows = out_0.rearrange("(p i) n -> p i n", i=PACK)
@@ -64,69 +64,68 @@ def tile_mix_three_tm_pl_mul_kernel(
         up_sc = new("up_sc", [P, M], U8)
         for plane in (w4_sc, w8_sc, up_sc):
             nc.vector.memset(plane[:].bitcast(I32), 0)
-        for q in range(QUADS):
+        for r in range(4):
             nc.gpsimd.dma_start(
-                out=w4_sc[32 * q : 32 * q + 4, :, :].bitcast(I32),
-                in_=w4_scales[:, 4 * q : 4 * q + 4, :].rearrange("a r n -> r a n").bitcast(I32),
+                out=w4_sc[r:P:32, :, :].bitcast(I32),
+                in_=w4_scales.rearrange("a (q r) n -> r q a n", r=4)[r].bitcast(I32),
             )
         for q in range(QUADS):
             nc.gpsimd.dma_start(
                 out=w8_sc[32 * q + W8_ROW : 32 * q + W8_ROW + 4 * W8_PASSES, :].bitcast(I32),
                 in_=w8_scales[:, 4 * q : 4 * q + 4, :].bitcast(I32),
             )
-        for q in range(QUADS):
+        for r in range(4):
             nc.gpsimd.dma_start(
-                out=up_sc[32 * q : 32 * q + 4, :].bitcast(I32),
-                in_=up_scales[0, 4 * q : 4 * q + 4, :].bitcast(I32),
+                out=up_sc[r:P:32, :].bitcast(I32),
+                in_=up_scales[0].rearrange("(q r) n -> r q n", r=4)[r].bitcast(I32),
             )
 
         order = [2, 3, 4, 0, 1]
         last = order[-1]
-        x_raw, d_raw, w8, w4, up = {}, {}, {}, {}, {}
+        x_raw, d_raw, w8, w4 = {}, {}, {}, [[], []]
         for a in order[:-1]:
             d_raw[a] = load_rows("d_raw%d" % a, down, a, 0, R)
             x_raw[a] = load_rows("x_raw%d" % a, x, a, 0, T)
             if a == 4:
-                w4[0] = load_fp4("w4", w4_words, 0)
+                w4[0].extend(load_fp4("w4_first", w4_words, 0, 1, 0, HALF))
         w8[0, 0] = load_w8(0, 0)
         d_raw[last] = load_rows("d_raw%d" % last, down, last, 0, R)
-        x_last = [load_rows("x_last%d" % u, x, last, u * T // 2, (u + 1) * T // 2) for u in range(2)]
+        w4[0].extend(load_fp4("w4_rest", w4_words, 1, W4_PASSES, 0, HALF))
+        x_raw[last] = load_rows("x_raw%d" % last, x, last, 0, T)
         w8[1, 0] = load_w8(1, 0)
-        up[0] = load_fp4("up", up_words, 0)
-        w4[1] = load_fp4("w4", w4_words, 1)
+        up = load_fp4("up", up_words, 0, 1, 0, M)[0]
+        w4[1].extend(load_fp4("w4_high", w4_words, 0, W4_PASSES, HALF, M))
         w8[0, 1] = load_w8(0, 1)
         w8[1, 1] = load_w8(1, 1)
-        g0 = []
+        g_sb = []
         for i in range(PACK):
-            g0.append(new("g0_%d" % i, [P, HALF], F32))
-            nc.sync.dma_start(out=g0[i][:], in_=g_rows[:, i, 0:HALF])
-            if i == 1:
-                up[1] = load_fp4("up", up_words, 1)
-        g1 = new("g1", [P, PACK, HALF], F32)
-        nc.sync.dma_start(out=g1[:], in_=g_rows[:, :, HALF:M])
+            g_sb.append(new("g%d" % i, [P, M], F32))
+            nc.sync.dma_start(out=g_sb[i][:], in_=g_rows[:, i, :])
 
-        def deal(dealt, halves):
-            dst = dealt[:].rearrange("p i m j -> p m i j")
-            for u, copy in ((0, nc.scalar.copy), (1, nc.vector.tensor_copy)):
-                copy(out=dst[:, 64 * u : 64 * (u + 1), :, :], in_=halves[u].rearrange("p j (m i) -> p m i j", i=PACK))
+        def deal(dealt, raw, by_block):
+            dst = dealt[:].rearrange("p i m j -> p m j i")
+            src = raw[:].rearrange("p j (m i) -> p m j i", i=PACK)
+            if by_block:
+                nc.vector.tensor_copy(out=dst[:, :, :, 0:2], in_=src[:, :, :, 0:2])
+                nc.scalar.copy(out=dst[:, :, :, 2:4], in_=src[:, :, :, 2:4])
+            else:
+                nc.scalar.copy(out=dst[:, 0:SCALAR_SHARE, :, :], in_=src[:, 0:SCALAR_SHARE, :, :])
+                nc.vector.tensor_copy(out=dst[:, SCALAR_SHARE:P, :, :], in_=src[:, SCALAR_SHARE:P, :, :])
 
         def quantize(codes, scales, values):
             nc.vector.quantize_mx(out=codes.bitcast(FP8X4), scales=scales, in_=values)
 
-        def prepare(name, halves, pieces):
+        def prepare(name, raw, pieces):
             dealt = new(name + "_bf", [P, PACK, P, PACK], BF16)
             codes = new(name + "_codes", [P, PACK * P], U32)
             scales = new(name + "_scales", [P, PACK * P], U8)
-            deal(dealt, halves)
+            deal(dealt, raw, pieces > 1)
             flat = dealt[:].rearrange("p i m j -> p (i m j)")
             width = PACK * P // pieces
             for c in range(pieces):
                 cols = slice(c * width, (c + 1) * width)
                 quantize(codes[:, cols], scales[:, cols], flat[:, PACK * c * width : PACK * (c + 1) * width])
             return codes, scales
-
-        def split(raw):
-            return [raw[:, :, 0:256], raw[:, :, 256:512]]
 
         h_ps = [ps.tile([P, PACK, P], F32, name="h_ps%d" % i, tag="bank%d" % i) for i in range(PACK)]
         y0_ps = [ps.tile([P, HALF], F32, name="y0_ps%d" % i, tag="bank%d" % (PACK + i)) for i in range(PACK)]
@@ -153,7 +152,7 @@ def tile_mix_three_tm_pl_mul_kernel(
             half, c0 = divmod(n0, HALF)
             if a == UP:
                 lhs, lhs_sc = hq[i][0][:], hq[i][1][:]
-                rhs = up[half][:, 0, 2 * c0 : 2 * (c0 + width)].bitcast(FP4X4)
+                rhs = up[:, 2 * n0 : 2 * (n0 + width)].bitcast(FP4X4)
                 rhs_sc = up_sc[:, n0 : n0 + width]
             else:
                 lhs, lhs_sc = xq[a][0][:, block(i)], xq[a][1][:, block(i)]
@@ -161,7 +160,7 @@ def tile_mix_three_tm_pl_mul_kernel(
                     rhs = w8[a, half][:, c0 : c0 + width].bitcast(FP8X4)
                     rhs_sc = w8_sc[W8_ROW + 4 * a : P, n0 : n0 + width]
                 else:
-                    rhs = w4[half][:, a - W8_PASSES, 2 * c0 : 2 * (c0 + width)].bitcast(FP4X4)
+                    rhs = w4[half][a - W8_PASSES][:, 2 * c0 : 2 * (c0 + width)].bitcast(FP4X4)
                     rhs_sc = w4_sc[:, a - W8_PASSES, n0 : n0 + width]
             nc.tensor.matmul_mx(
                 out=out, lhsT=lhs.bitcast(FP8X4), lhsT_scale=lhs_sc, rhs=rhs, rhs_scale=rhs_sc, start=start, stop=stop
@@ -172,16 +171,16 @@ def tile_mix_three_tm_pl_mul_kernel(
                 y_pass(y0_ps[i][:], a, i, 0, HALF, a == order[0], a == UP)
 
         for a in order[:-1]:
-            dq[a] = prepare("d%d" % a, split(d_raw[a]), 1)
-            xq[a] = prepare("x%d" % a, split(x_raw[a]), 1)
+            dq[a] = prepare("d%d" % a, d_raw[a], 1)
+            xq[a] = prepare("x%d" % a, x_raw[a], 1)
             for i in range(PACK):
                 h_pass(a, i)
             if a == 4:
-                for b in order[:3]:
-                    y0_pass(b)
-        y0_pass(0)
-        dq[last] = prepare("d%d" % last, split(d_raw[last]), 1)
-        xq[last] = prepare("x%d" % last, [half[:] for half in x_last], PACK)
+                y0_pass(2)
+        for a in (0, 3, 4):
+            y0_pass(a)
+        dq[last] = prepare("d%d" % last, d_raw[last], 1)
+        xq[last] = prepare("x%d" % last, x_raw[last], PACK)
         for i in range(PACK):
             h_pass(last, i)
         y0_pass(last)
@@ -207,18 +206,20 @@ def tile_mix_three_tm_pl_mul_kernel(
         y0_pass(UP)
 
         y1_ps = []
-        for c in range(PACK):
-            y1_ps.append(ps.tile([P, PACK, P], F32, name="y1_ps%d" % c, tag="bank%d" % c))
-            for i in range(PACK):
-                for a in order + [UP]:
-                    y_pass(y1_ps[c][:, i, :], a, i, HALF + c * P, P, a == order[0], a == UP)
+        for i in range(PACK):
+            y1_ps.append(ps.tile([P, HALF], F32, name="y1_ps%d" % i, tag="bank%d" % i))
+            for a in order + [UP]:
+                y_pass(y1_ps[i][:], a, i, HALF, HALF, a == order[0], a == UP)
 
         o_words = new("o_words", [P, M], U32)
         o_scales = new("o_scales", [P, M], U8)
 
-        def interleave(name, res, c0, width, copy):
+        def interleave(name, res_half, c0, width, copy):
             o_bf = new(name, [P, width, PACK], BF16)
-            copy(out=o_bf[:], in_=res[:, :, c0 : c0 + width].rearrange("p i n -> p n i"))
+            copy(
+                out=o_bf[:].rearrange("p (c e) i -> p c i e", e=4),
+                in_=res_half[:, :, c0 : c0 + width].rearrange("p i (c e) -> p c i e", e=4),
+            )
             return o_bf
 
         def o_quant(o_bf, n0):
@@ -228,39 +229,45 @@ def tile_mix_three_tm_pl_mul_kernel(
         def store_words(n0, n1):
             nc.sync.dma_start(out=out_words[:, 4 * n0 : 4 * n1].bitcast(I32), in_=o_words[:, n0:n1].bitcast(I32))
 
-        def mul1(res, c0, c):
-            nc.vector.tensor_tensor(out=res[:, :, c0 : c0 + P], in0=y1_ps[c][:], in1=g1[:, :, block(c)], op=MULT)
+        res = [new("res%d" % half, [P, PACK, HALF], F32) for half in range(2)]
+        y_ps = [y0_ps, y1_ps]
 
-        res0 = new("res0", [P, PACK, HALF], F32)
-        for i in range(PACK):
-            nc.vector.tensor_tensor(out=res0[:, i, :], in0=y0_ps[i][:], in1=g0[i][:], op=MULT)
-            nc.sync.dma_start(out=out_rows[:, i, 0:HALF], in_=res0[:, i, :])
-        res1a = new("res1a", [P, PACK, 2 * P], F32)
-        res1b = new("res1b", [P, PACK, P], F32)
-        res1c = new("res1c", [P, PACK, P], F32)
+        def mul(half, i, c0, c1):
+            n0 = half * HALF
+            nc.vector.tensor_tensor(
+                out=res[half][:, i, c0:c1], in0=y_ps[half][i][:, c0:c1], in1=g_sb[i][:, n0 + c0 : n0 + c1], op=MULT
+            )
 
-        bf0b = interleave("bf0b", res0, 256, 256, nc.scalar.copy)
-        mul1(res1a, 0, 0)
-        bf0a = interleave("bf0a", res0, 0, 256, nc.vector.tensor_copy)
-        mul1(res1a, P, 1)
-        nc.sync.dma_start(out=out_rows[:, :, HALF : HALF + 2 * P], in_=res1a[:])
-        bf1a = interleave("bf1a", res1a, 0, 256, nc.scalar.copy)
+        def store(half, i):
+            nc.sync.dma_start(out=out_rows[:, i, half * HALF : (half + 1) * HALF], in_=res[half][:, i, :])
+
+        def finish(half, i):
+            mul(half, i, 0, HALF)
+            store(half, i)
+
+        finish(0, 0)
+        finish(0, 1)
+        finish(1, 0)
+        finish(0, 2)
+        finish(0, 3)
+        bf0a = interleave("bf0a", res[0], 0, 256, nc.scalar.copy)
+        finish(1, 1)
+        bf0b = interleave("bf0b", res[0], 256, 256, nc.vector.tensor_copy)
+        finish(1, 2)
         o_quant(bf0a, 0)
         o_quant(bf0b, 256)
         store_words(0, HALF)
-        mul1(res1b, 0, 2)
-        nc.sync.dma_start(out=out_rows[:, :, HALF + 2 * P : HALF + 3 * P], in_=res1b[:])
-        bf1b = interleave("bf1b", res1b, 0, P, nc.scalar.copy)
+        mul(1, 3, 0, 256)
+        bf1a = interleave("bf1a", res[1], 0, 256, nc.scalar.copy)
+        mul(1, 3, 256, HALF)
+        store(1, 3)
+        bf1b = interleave("bf1b", res[1], 256, 256, nc.vector.tensor_copy)
+        o_quant(bf1b, HALF + 256)
+        store_words(HALF + 256, M)
         o_quant(bf1a, HALF)
-        o_quant(bf1b, HALF + 2 * P)
-        store_words(HALF, HALF + 3 * P)
-        mul1(res1c, 0, 3)
-        nc.sync.dma_start(out=out_rows[:, :, HALF + 3 * P : M], in_=res1c[:])
-        bf1c = interleave("bf1c", res1c, 0, P, nc.vector.tensor_copy)
-        o_quant(bf1c, HALF + 3 * P)
-        store_words(HALF + 3 * P, M)
-        for q in range(QUADS):
-            queue = nc.scalar if q % 2 == 0 else nc.sync
+        store_words(HALF, HALF + 256)
+        for r in range(4):
+            queue = nc.scalar if r % 2 == 0 else nc.sync
             queue.dma_start(
-                out=out_2[0, 4 * q : 4 * q + 4, :].bitcast(I32), in_=o_scales[32 * q : 32 * q + 4, :].bitcast(I32)
+                out=out_2[0].rearrange("(q r) n -> r q n", r=4)[r].bitcast(I32), in_=o_scales[r:P:32, :].bitcast(I32)
             )

@@ -37,17 +37,17 @@ def tile_mix_three_tm_pl_mul_kernel(
         def new(name, shape, dtype):
             return sb.tile(shape, dtype, name=name, align_bytes=64)
 
-        def load_rows(name, src, a, c0, c1):
-            raw = new(name, [P, PACK, c1 - c0], F32)
-            rows = src[a * K_PASS : (a + 1) * K_PASS, :].rearrange("(p j) c -> p j c", j=PACK)
-            nc.sync.dma_start(out=raw[:], in_=rows[:, :, c0:c1])
-            return raw
+        def load_rows(name, src, a0, a1):
+            raw = new(name, [P, a1 - a0, PACK, src.shape[1]], F32)
+            rows = src[a0 * K_PASS : a1 * K_PASS, :].rearrange("(a p j) c -> p a (j c)", p=P, j=PACK)
+            nc.sync.dma_start(out=raw[:].rearrange("p a j c -> p a (j c)"), in_=rows)
+            return {a: raw[:, a - a0, :, :] for a in range(a0, a1)}
 
-        def load_w8(a, half):
-            words = new("w8_%d_%d" % (a, half), [P, HALF], U32)
-            src = w8_words[a].rearrange("p n i -> p (n i)")[:, half * 4 * HALF : (half + 1) * 4 * HALF]
+        def load_w8(a0, a1, half):
+            words = new("w8_%d_%d" % (a0, half), [P, a1 - a0, HALF], U32)
+            src = w8_words.rearrange("a p n i -> p a (n i)")[:, a0:a1, half * 4 * HALF : (half + 1) * 4 * HALF]
             nc.sync.dma_start(out=words[:].bitcast(I32), in_=src.bitcast(I32))
-            return words
+            return [words[:, a, :] for a in range(a1 - a0)]
 
         def load_fp4(name, src_words, a0, a1, n0, n1):
             words = new(name, [P, a1 - a0, 2 * (n1 - n0)], U8)
@@ -82,29 +82,32 @@ def tile_mix_three_tm_pl_mul_kernel(
 
         order = [2, 3, 4, 0, 1]
         last = order[-1]
-        x_raw, d_raw, w8, w4 = {}, {}, {}, [[], []]
-        for a in order[:-1]:
-            d_raw[a] = load_rows("d_raw%d" % a, down, a, 0, R)
-            x_raw[a] = load_rows("x_raw%d" % a, x, a, 0, T)
-            if a == 4:
-                w4[0].extend(load_fp4("w4_first", w4_words, 0, 1, 0, HALF))
-        w8[0, 0] = load_w8(0, 0)
-        d_raw[last] = load_rows("d_raw%d" % last, down, last, 0, R)
+        w8, w4 = [[], []], [[], []]
+        d_loads = [load_rows("d_raw2", down, 2, 4)]
+        x_loads = [load_rows("x_raw2", x, 2, 4)]
+        d_loads.append(load_rows("d_raw4", down, 4, 5))
+        x_loads.append(load_rows("x_raw4", x, 4, 5))
+        w4[0].extend(load_fp4("w4_first", w4_words, 0, 1, 0, HALF))
+        d_loads.append(load_rows("d_raw0", down, 0, 1))
+        x_loads.append(load_rows("x_raw0", x, 0, 1))
+        w8[0].extend(load_w8(0, 1, 0))
+        d_loads.append(load_rows("d_raw1", down, 1, 2))
         w4[0].extend(load_fp4("w4_rest", w4_words, 1, W4_PASSES, 0, HALF))
-        x_raw[last] = load_rows("x_raw%d" % last, x, last, 0, T)
-        w8[1, 0] = load_w8(1, 0)
+        x_loads.append(load_rows("x_raw1", x, 1, 2))
+        w8[0].extend(load_w8(1, 2, 0))
         up = load_fp4("up", up_words, 0, 1, 0, M)[0]
         w4[1].extend(load_fp4("w4_high", w4_words, 0, W4_PASSES, HALF, M))
-        w8[0, 1] = load_w8(0, 1)
-        w8[1, 1] = load_w8(1, 1)
-        g_sb = []
-        for i in range(PACK):
-            g_sb.append(new("g%d" % i, [P, M], F32))
-            nc.sync.dma_start(out=g_sb[i][:], in_=g_rows[:, i, :])
+        w8[1].extend(load_w8(0, W8_PASSES, 1))
+        g_sb = [[], []]
+        for half in range(2):
+            for i0 in (0, 2):
+                pair = new("g%d_%d" % (half, i0), [P, 2, HALF], F32)
+                nc.sync.dma_start(out=pair[:], in_=g_rows[:, i0 : i0 + 2, half * HALF : (half + 1) * HALF])
+                g_sb[half].extend([pair[:, 0, :], pair[:, 1, :]])
 
         def deal(dealt, raw, by_block):
             dst = dealt[:].rearrange("p i m j -> p m j i")
-            src = raw[:].rearrange("p j (m i) -> p m j i", i=PACK)
+            src = raw.rearrange("p j (m i) -> p m j i", i=PACK)
             if by_block:
                 nc.vector.tensor_copy(out=dst[:, :, :, 0:2], in_=src[:, :, :, 0:2])
                 nc.scalar.copy(out=dst[:, :, :, 2:4], in_=src[:, :, :, 2:4])
@@ -157,7 +160,7 @@ def tile_mix_three_tm_pl_mul_kernel(
             else:
                 lhs, lhs_sc = xq[a][0][:, block(i)], xq[a][1][:, block(i)]
                 if a < W8_PASSES:
-                    rhs = w8[a, half][:, c0 : c0 + width].bitcast(FP8X4)
+                    rhs = w8[half][a][:, c0 : c0 + width].bitcast(FP8X4)
                     rhs_sc = w8_sc[W8_ROW + 4 * a : P, n0 : n0 + width]
                 else:
                     rhs = w4[half][a - W8_PASSES][:, 2 * c0 : 2 * (c0 + width)].bitcast(FP4X4)
@@ -170,17 +173,19 @@ def tile_mix_three_tm_pl_mul_kernel(
             for i in range(PACK):
                 y_pass(y0_ps[i][:], a, i, 0, HALF, a == order[0], a == UP)
 
-        for a in order[:-1]:
-            dq[a] = prepare("d%d" % a, d_raw[a], 1)
-            xq[a] = prepare("x%d" % a, x_raw[a], 1)
-            for i in range(PACK):
-                h_pass(a, i)
-            if a == 4:
-                y0_pass(2)
+        for d_raw, x_raw in zip(d_loads[:-1], x_loads[:-1]):
+            for a in d_raw:
+                dq[a] = prepare("d%d" % a, d_raw[a], 1)
+            for a in x_raw:
+                xq[a] = prepare("x%d" % a, x_raw[a], 1)
+                for i in range(PACK):
+                    h_pass(a, i)
+                if a == 4:
+                    y0_pass(2)
         for a in (0, 3, 4):
             y0_pass(a)
-        dq[last] = prepare("d%d" % last, d_raw[last], 1)
-        xq[last] = prepare("x%d" % last, x_raw[last], PACK)
+        dq[last] = prepare("d%d" % last, d_loads[-1][last], 1)
+        xq[last] = prepare("x%d" % last, x_loads[-1][last], PACK)
         for i in range(PACK):
             h_pass(last, i)
         y0_pass(last)
@@ -206,7 +211,7 @@ def tile_mix_three_tm_pl_mul_kernel(
         y0_pass(UP)
 
         y1_ps = []
-        for i in range(PACK):
+        for i in range(PACK - 1):
             y1_ps.append(ps.tile([P, HALF], F32, name="y1_ps%d" % i, tag="bank%d" % i))
             for a in order + [UP]:
                 y_pass(y1_ps[i][:], a, i, HALF, HALF, a == order[0], a == UP)
@@ -230,42 +235,50 @@ def tile_mix_three_tm_pl_mul_kernel(
             nc.sync.dma_start(out=out_words[:, 4 * n0 : 4 * n1].bitcast(I32), in_=o_words[:, n0:n1].bitcast(I32))
 
         res = [new("res%d" % half, [P, PACK, HALF], F32) for half in range(2)]
-        y_ps = [y0_ps, y1_ps]
 
-        def mul(half, i, c0, c1):
-            n0 = half * HALF
-            nc.vector.tensor_tensor(
-                out=res[half][:, i, c0:c1], in0=y_ps[half][i][:, c0:c1], in1=g_sb[i][:, n0 + c0 : n0 + c1], op=MULT
-            )
+        def mul(half, i, c0, c1, y):
+            nc.vector.tensor_tensor(out=res[half][:, i, c0:c1], in0=y, in1=g_sb[half][i][:, c0:c1], op=MULT)
 
-        def store(half, i):
-            nc.sync.dma_start(out=out_rows[:, i, half * HALF : (half + 1) * HALF], in_=res[half][:, i, :])
+        def store(half, i0, i1):
+            nc.sync.dma_start(out=out_rows[:, i0:i1, half * HALF : (half + 1) * HALF], in_=res[half][:, i0:i1, :])
 
-        def finish(half, i):
-            mul(half, i, 0, HALF)
-            store(half, i)
+        for i in range(PACK):
+            mul(0, i, 0, HALF, y0_ps[i][:])
+        store(0, 0, PACK)
 
-        finish(0, 0)
-        finish(0, 1)
-        finish(1, 0)
-        finish(0, 2)
-        finish(0, 3)
+        end_ps = []
+        for c in range(PACK):
+            end_ps.append(ps.tile([P, HALF], F32, name="end_ps%d" % c, tag="bank%d" % (PACK + c)))
+            for a in order + [UP]:
+                y_pass(end_ps[c][:, 0:P], a, PACK - 1, HALF + c * P, P, a == order[0], a == UP)
+
+        def mul_end(c):
+            mul(1, PACK - 1, c * P, (c + 1) * P, end_ps[c][:, 0:P])
+
         bf0a = interleave("bf0a", res[0], 0, 256, nc.scalar.copy)
-        finish(1, 1)
         bf0b = interleave("bf0b", res[0], 256, 256, nc.vector.tensor_copy)
-        finish(1, 2)
+        mul(1, 0, 0, HALF, y1_ps[0][:])
         o_quant(bf0a, 0)
         o_quant(bf0b, 256)
         store_words(0, HALF)
-        mul(1, 3, 0, 256)
-        bf1a = interleave("bf1a", res[1], 0, 256, nc.scalar.copy)
-        mul(1, 3, 256, HALF)
-        store(1, 3)
-        bf1b = interleave("bf1b", res[1], 256, 256, nc.vector.tensor_copy)
-        o_quant(bf1b, HALF + 256)
-        store_words(HALF + 256, M)
-        o_quant(bf1a, HALF)
-        store_words(HALF, HALF + 256)
+        mul(1, 1, 0, HALF, y1_ps[1][:])
+        store(1, 0, 2)
+        mul(1, 2, 0, HALF, y1_ps[2][:])
+        store(1, 2, 3)
+        mul_end(0)
+        bf10 = interleave("bf10", res[1], 0, P, nc.scalar.copy)
+        mul_end(1)
+        bf11 = interleave("bf11", res[1], P, P, nc.scalar.copy)
+        mul_end(2)
+        o_quant(bf10, HALF)
+        mul_end(3)
+        store(1, 3, 4)
+        bf13 = interleave("bf13", res[1], 3 * P, P, nc.scalar.copy)
+        bf12 = interleave("bf12", res[1], 2 * P, P, nc.vector.tensor_copy)
+        o_quant(bf11, HALF + P)
+        o_quant(bf12, HALF + 2 * P)
+        o_quant(bf13, HALF + 3 * P)
+        store_words(HALF, M)
         for r in range(4):
             queue = nc.scalar if r % 2 == 0 else nc.sync
             queue.dma_start(

@@ -23,6 +23,7 @@ W4_PASSES = (K - O) // K_PASS
 QUADS = 4
 W8_ROW = 4
 SCALAR_SHARE = 56
+LOW_SCALAR_COLS = 320
 
 
 def tile_mix_three_tm_pl_mul_kernel(
@@ -59,25 +60,26 @@ def tile_mix_three_tm_pl_mul_kernel(
         out_rows = out_0.rearrange("(p i) n -> p i n", i=PACK)
         out_words = out_1[0].rearrange("p n i -> p (n i)")
 
-        w4_sc = new("w4_sc", [P, W4_PASSES, M], U8)
+        w4_sc = [new("w4_sc%d" % half, [P, W4_PASSES, HALF], U8) for half in range(2)]
         w8_sc = new("w8_sc", [P, M], U8)
         up_sc = new("up_sc", [P, M], U8)
-        for plane in (w4_sc, w8_sc, up_sc):
+        for plane in (w4_sc[0], w8_sc, up_sc, w4_sc[1]):
             nc.vector.memset(plane[:].bitcast(I32), 0)
+
+        def load_w4_scales(queue, half, r):
+            src = w4_scales.rearrange("a (q r) n -> r q a n", r=4)[r][:, :, half * HALF : (half + 1) * HALF]
+            queue.dma_start(out=w4_sc[half][r:P:32, :, :].bitcast(I32), in_=src.bitcast(I32))
+
+        def load_up_scales(r):
+            src = up_scales[0].rearrange("(q r) n -> r q n", r=4)[r]
+            nc.sync.dma_start(out=up_sc[r:P:32, :].bitcast(I32), in_=src.bitcast(I32))
+
         for r in range(4):
-            nc.gpsimd.dma_start(
-                out=w4_sc[r:P:32, :, :].bitcast(I32),
-                in_=w4_scales.rearrange("a (q r) n -> r q a n", r=4)[r].bitcast(I32),
-            )
+            load_w4_scales(nc.gpsimd, 0, r)
         for q in range(QUADS):
             nc.gpsimd.dma_start(
                 out=w8_sc[32 * q + W8_ROW : 32 * q + W8_ROW + 4 * W8_PASSES, :].bitcast(I32),
                 in_=w8_scales[:, 4 * q : 4 * q + 4, :].bitcast(I32),
-            )
-        for r in range(4):
-            nc.gpsimd.dma_start(
-                out=up_sc[r:P:32, :].bitcast(I32),
-                in_=up_scales[0].rearrange("(q r) n -> r q n", r=4)[r].bitcast(I32),
             )
 
         order = [2, 3, 4, 0, 1]
@@ -95,9 +97,17 @@ def tile_mix_three_tm_pl_mul_kernel(
         w4[0].extend(load_fp4("w4_rest", w4_words, 1, W4_PASSES, 0, HALF))
         x_loads.append(load_rows("x_raw1", x, 1, 2))
         w8[0].extend(load_w8(1, 2, 0))
+        load_up_scales(0)
+        load_up_scales(1)
         up = load_fp4("up", up_words, 0, 1, 0, M)[0]
+        load_up_scales(2)
+        load_up_scales(3)
         w4[1].extend(load_fp4("w4_high", w4_words, 0, W4_PASSES, HALF, M))
+        load_w4_scales(nc.sync, 1, 0)
+        load_w4_scales(nc.sync, 1, 1)
         w8[1].extend(load_w8(0, W8_PASSES, 1))
+        load_w4_scales(nc.sync, 1, 2)
+        load_w4_scales(nc.sync, 1, 3)
         g_sb = [[], []]
         for half in range(2):
             for i0 in (0, 2):
@@ -164,7 +174,7 @@ def tile_mix_three_tm_pl_mul_kernel(
                     rhs_sc = w8_sc[W8_ROW + 4 * a : P, n0 : n0 + width]
                 else:
                     rhs = w4[half][a - W8_PASSES][:, 2 * c0 : 2 * (c0 + width)].bitcast(FP4X4)
-                    rhs_sc = w4_sc[:, a - W8_PASSES, n0 : n0 + width]
+                    rhs_sc = w4_sc[half][:, a - W8_PASSES, c0 : c0 + width]
             nc.tensor.matmul_mx(
                 out=out, lhsT=lhs.bitcast(FP8X4), lhsT_scale=lhs_sc, rhs=rhs, rhs_scale=rhs_sc, start=start, stop=stop
             )
@@ -255,14 +265,17 @@ def tile_mix_three_tm_pl_mul_kernel(
         def mul_end(c):
             mul(1, PACK - 1, c * P, (c + 1) * P, end_ps[c][:, 0:P])
 
-        bf0a = interleave("bf0a", res[0], 0, 256, nc.scalar.copy)
-        bf0b = interleave("bf0b", res[0], 256, 256, nc.vector.tensor_copy)
+        bf0 = new("bf0", [P, HALF, PACK], BF16)
+        for c0, c1, copy in ((0, LOW_SCALAR_COLS, nc.scalar.copy), (LOW_SCALAR_COLS, HALF, nc.vector.tensor_copy)):
+            copy(
+                out=bf0[:, c0:c1, :].rearrange("p (c e) i -> p c i e", e=4),
+                in_=res[0][:, :, c0:c1].rearrange("p i (c e) -> p c i e", e=4),
+            )
         mul(1, 0, 0, HALF, y1_ps[0][:])
-        o_quant(bf0a, 0)
-        o_quant(bf0b, 256)
-        store_words(0, HALF)
         mul(1, 1, 0, HALF, y1_ps[1][:])
         store(1, 0, 2)
+        o_quant(bf0, 0)
+        store_words(0, HALF)
         mul(1, 2, 0, HALF, y1_ps[2][:])
         store(1, 2, 3)
         mul_end(0)

from contextlib import ExitStack

import concourse.mybir as mybir

O, K, R, M, T = 1024, 2560, 512, 1024, 512
FLOPS = 2 * (K * R * T + K * T * M + R * T * M)

F32 = mybir.dt.float32
BF16 = mybir.dt.bfloat16
I32 = mybir.dt.int32
U32 = mybir.dt.uint32
U8 = mybir.dt.uint8
FP8X4 = mybir.dt.float8_e4m3fn_x4
FP4X4 = mybir.dt.float4_e2m1fn_x4
MULT = mybir.AluOpType.mult

P = 128
PACK = 4
K_PASS = P * PACK
HALF = M // 2
W8_PASSES = O // K_PASS
W4_PASSES = (K - O) // K_PASS
QUADS = 4
W8_ROW = 4
SCALAR_SHARE = 56
LOW_SCALAR_COLS = 320


def tile_mix_three_tm_pl_mul_kernel(
    tc, x, w8_words, w8_scales, w4_words, w4_scales, down, up_words, up_scales, g, out_0, out_1, out_2
):
    nc = tc.nc
    with ExitStack() as ctx:
        sb = ctx.enter_context(tc.tile_pool(name="sb", bufs=1))
        ps = ctx.enter_context(tc.psum_pool(name="ps", bufs=1))
        ctx.enter_context(tc.manual_schedule())

        def new(name, shape, dtype):
            return sb.tile(shape, dtype, name=name, align_bytes=64)

        def load_rows(name, src, a0, a1):
            raw = new(name, [P, a1 - a0, PACK, src.shape[1]], F32)
            rows = src[a0 * K_PASS : a1 * K_PASS, :].rearrange("(a p j) c -> p a (j c)", p=P, j=PACK)
            nc.sync.dma_start(out=raw[:].rearrange("p a j c -> p a (j c)"), in_=rows)
            return {a: raw[:, a - a0, :, :] for a in range(a0, a1)}

        def load_w8(a0, a1, half):
            words = new("w8_%d_%d" % (a0, half), [P, a1 - a0, HALF], U32)
            src = w8_words.rearrange("a p n i -> p a (n i)")[:, a0:a1, half * 4 * HALF : (half + 1) * 4 * HALF]
            nc.sync.dma_start(out=words[:].bitcast(I32), in_=src.bitcast(I32))
            return [words[:, a, :] for a in range(a1 - a0)]

        def load_fp4(name, src_words, a0, a1, n0, n1):
            words = new(name, [P, a1 - a0, 2 * (n1 - n0)], U8)
            src = src_words.rearrange("a p c -> p a c")[:, a0:a1, 2 * n0 : 2 * n1]
            nc.sync.dma_start(out=words[:].bitcast(I32), in_=src.bitcast(I32))
            return [words[:, a, :] for a in range(a1 - a0)]

        g_rows = g.rearrange("(p i) n -> p i n", i=PACK)
        out_rows = out_0.rearrange("(p i) n -> p i n", i=PACK)
        out_words = out_1[0].rearrange("p n i -> p (n i)")

        w4_sc = [new("w4_sc%d" % half, [P, W4_PASSES, HALF], U8) for half in range(2)]
        w8_sc = new("w8_sc", [P, M], U8)
        up_sc = new("up_sc", [P, M], U8)
        for plane in (w4_sc[0], w8_sc, up_sc, w4_sc[1]):
            nc.vector.memset(plane[:].bitcast(I32), 0)

        def load_w4_scales(queue, half, r):
            src = w4_scales.rearrange("a (q r) n -> r q a n", r=4)[r][:, :, half * HALF : (half + 1) * HALF]
            queue.dma_start(out=w4_sc[half][r:P:32, :, :].bitcast(I32), in_=src.bitcast(I32))

        def load_up_scales(r):
            src = up_scales[0].rearrange("(q r) n -> r q n", r=4)[r]
            nc.sync.dma_start(out=up_sc[r:P:32, :].bitcast(I32), in_=src.bitcast(I32))

        for r in range(4):
            load_w4_scales(nc.gpsimd, 0, r)
        for q in range(QUADS):
            nc.gpsimd.dma_start(
                out=w8_sc[32 * q + W8_ROW : 32 * q + W8_ROW + 4 * W8_PASSES, :].bitcast(I32),
                in_=w8_scales[:, 4 * q : 4 * q + 4, :].bitcast(I32),
            )

        order = [2, 3, 4, 0, 1]
        last = order[-1]
        w8, w4 = [[], []], [[], []]
        d_loads = [load_rows("d_raw2", down, 2, 4)]
        x_loads = [load_rows("x_raw2", x, 2, 4)]
        d_loads.append(load_rows("d_raw4", down, 4, 5))
        x_loads.append(load_rows("x_raw4", x, 4, 5))
        w4[0].extend(load_fp4("w4_first", w4_words, 0, 1, 0, HALF))
        d_loads.append(load_rows("d_raw0", down, 0, 1))
        x_loads.append(load_rows("x_raw0", x, 0, 1))
        w8[0].extend(load_w8(0, 1, 0))
        d_loads.append(load_rows("d_raw1", down, 1, 2))
        w4[0].extend(load_fp4("w4_rest", w4_words, 1, W4_PASSES, 0, HALF))
        x_loads.append(load_rows("x_raw1", x, 1, 2))
        w8[0].extend(load_w8(1, 2, 0))
        load_up_scales(0)
        load_up_scales(1)
        up = load_fp4("up", up_words, 0, 1, 0, M)[0]
        load_up_scales(2)
        load_up_scales(3)
        w4[1].extend(load_fp4("w4_high", w4_words, 0, W4_PASSES, HALF, M))
        load_w4_scales(nc.sync, 1, 0)
        load_w4_scales(nc.sync, 1, 1)
        w8[1].extend(load_w8(0, W8_PASSES, 1))
        load_w4_scales(nc.sync, 1, 2)
        load_w4_scales(nc.sync, 1, 3)
        g_sb = [[], []]
        for half in range(2):
            for i0 in (0, 2):
                pair = new("g%d_%d" % (half, i0), [P, 2, HALF], F32)
                nc.sync.dma_start(out=pair[:], in_=g_rows[:, i0 : i0 + 2, half * HALF : (half + 1) * HALF])
                g_sb[half].extend([pair[:, 0, :], pair[:, 1, :]])

        def deal(dealt, raw, by_block):
            dst = dealt[:].rearrange("p i m j -> p m j i")
            src = raw.rearrange("p j (m i) -> p m j i", i=PACK)
            if by_block:
                nc.vector.tensor_copy(out=dst[:, :, :, 0:2], in_=src[:, :, :, 0:2])
                nc.scalar.copy(out=dst[:, :, :, 2:4], in_=src[:, :, :, 2:4])
            else:
                nc.scalar.copy(out=dst[:, 0:SCALAR_SHARE, :, :], in_=src[:, 0:SCALAR_SHARE, :, :])
                nc.vector.tensor_copy(out=dst[:, SCALAR_SHARE:P, :, :], in_=src[:, SCALAR_SHARE:P, :, :])

        def quantize(codes, scales, values):
            nc.vector.quantize_mx(out=codes.bitcast(FP8X4), scales=scales, in_=values)

        def prepare(name, raw, pieces):
            dealt = new(name + "_bf", [P, PACK, P, PACK], BF16)
            codes = new(name + "_codes", [P, PACK * P], U32)
            scales = new(name + "_scales", [P, PACK * P], U8)
            deal(dealt, raw, pieces > 1)
            flat = dealt[:].rearrange("p i m j -> p (i m j)")
            width = PACK * P // pieces
            for c in range(pieces):
                cols = slice(c * width, (c + 1) * width)
                quantize(codes[:, cols], scales[:, cols], flat[:, PACK * c * width : PACK * (c + 1) * width])
            return codes, scales

        h_ps = [ps.tile([P, PACK, P], F32, name="h_ps%d" % i, tag="bank%d" % i) for i in range(PACK)]
        y0_ps = [ps.tile([P, HALF], F32, name="y0_ps%d" % i, tag="bank%d" % (PACK + i)) for i in range(PACK)]
        xq, dq, hq = {}, {}, {}

        def block(i):
            return slice(i * P, (i + 1) * P)

        def h_pass(a, i):
            for j in range(PACK):
                nc.tensor.matmul_mx(
                    out=h_ps[i][:, j, :],
                    lhsT=dq[a][0][:, block(j)].bitcast(FP8X4),
                    lhsT_scale=dq[a][1][:, block(j)],
                    rhs=xq[a][0][:, block(i)].bitcast(FP8X4),
                    rhs_scale=xq[a][1][:, block(i)],
                    start=(a == order[0] and j == 0),
                    stop=(a == last and j == PACK - 1),
                )

        UP = "up"

        def y_pass(out, a, i, n0, width, start, stop):
            half, c0 = divmod(n0, HALF)
            if a == UP:
                lhs, lhs_sc = hq[i][0][:], hq[i][1][:]
                rhs = up[:, 2 * n0 : 2 * (n0 + width)].bitcast(FP4X4)
                rhs_sc = up_sc[:, n0 : n0 + width]
            else:
                lhs, lhs_sc = xq[a][0][:, block(i)], xq[a][1][:, block(i)]
                if a < W8_PASSES:
                    rhs = w8[half][a][:, c0 : c0 + width].bitcast(FP8X4)
                    rhs_sc = w8_sc[W8_ROW + 4 * a : P, n0 : n0 + width]
                else:
                    rhs = w4[half][a - W8_PASSES][:, 2 * c0 : 2 * (c0 + width)].bitcast(FP4X4)
                    rhs_sc = w4_sc[half][:, a - W8_PASSES, c0 : c0 + width]
            nc.tensor.matmul_mx(
                out=out, lhsT=lhs.bitcast(FP8X4), lhsT_scale=lhs_sc, rhs=rhs, rhs_scale=rhs_sc, start=start, stop=stop
            )

        def y0_pass(a):
            for i in range(PACK):
                y_pass(y0_ps[i][:], a, i, 0, HALF, a == order[0], a == UP)

        for d_raw, x_raw in zip(d_loads[:-1], x_loads[:-1]):
            for a in d_raw:
                dq[a] = prepare("d%d" % a, d_raw[a], 1)
            for a in x_raw:
                xq[a] = prepare("x%d" % a, x_raw[a], 1)
                for i in range(PACK):
                    h_pass(a, i)
                if a == 4:
                    y0_pass(2)
        for a in (0, 3, 4):
            y0_pass(a)
        dq[last] = prepare("d%d" % last, d_loads[-1][last], 1)
        xq[last] = prepare("x%d" % last, x_loads[-1][last], PACK)
        for i in range(PACK):
            h_pass(last, i)
        y0_pass(last)

        h_bf = [new("h_bf%d" % i, [P, P, PACK], BF16) for i in range(PACK)]
        for i in range(PACK):
            hq[i] = (new("h_codes%d" % i, [P, P], U32), new("h_scales%d" % i, [P, P], U8))

        def h_out(i, copy):
            copy(out=h_bf[i][:], in_=h_ps[i][:].rearrange("p j t -> p t j"))

        def h_quant(i):
            quantize(hq[i][0][:], hq[i][1][:], h_bf[i][:].rearrange("p t j -> p (t j)"))

        h_out(0, nc.scalar.copy)
        h_out(1, nc.vector.tensor_copy)
        h_out(2, nc.scalar.copy)
        h_quant(0)
        h_quant(1)
        h_out(3, nc.vector.tensor_copy)
        h_quant(2)
        h_quant(3)
        y0_pass(UP)

        y1_ps = []
        for i in range(PACK - 1):
            y1_ps.append(ps.tile([P, HALF], F32, name="y1_ps%d" % i, tag="bank%d" % i))
            for a in order + [UP]:
                y_pass(y1_ps[i][:], a, i, HALF, HALF, a == order[0], a == UP)

        o_words = new("o_words", [P, M], U32)
        o_scales = new("o_scales", [P, M], U8)

        def interleave(name, res_half, c0, width, copy):
            o_bf = new(name, [P, width, PACK], BF16)
            copy(
                out=o_bf[:].rearrange("p (c e) i -> p c i e", e=4),
                in_=res_half[:, :, c0 : c0 + width].rearrange("p i (c e) -> p c i e", e=4),
            )
            return o_bf

        def o_quant(o_bf, n0):
            cols = slice(n0, n0 + o_bf.shape[1])
            quantize(o_words[:, cols], o_scales[:, cols], o_bf[:].rearrange("p n i -> p (n i)"))

        def store_words(n0, n1):
            nc.sync.dma_start(out=out_words[:, 4 * n0 : 4 * n1].bitcast(I32), in_=o_words[:, n0:n1].bitcast(I32))

        res = [new("res%d" % half, [P, PACK, HALF], F32) for half in range(2)]

        def mul(half, i, c0, c1, y):
            nc.vector.tensor_tensor(out=res[half][:, i, c0:c1], in0=y, in1=g_sb[half][i][:, c0:c1], op=MULT)

        def store(half, i0, i1):
            nc.sync.dma_start(out=out_rows[:, i0:i1, half * HALF : (half + 1) * HALF], in_=res[half][:, i0:i1, :])

        for i in range(PACK):
            mul(0, i, 0, HALF, y0_ps[i][:])
        store(0, 0, PACK)

        end_ps = []
        for c in range(PACK):
            end_ps.append(ps.tile([P, HALF], F32, name="end_ps%d" % c, tag="bank%d" % (PACK + c)))
            for a in order + [UP]:
                y_pass(end_ps[c][:, 0:P], a, PACK - 1, HALF + c * P, P, a == order[0], a == UP)

        def mul_end(c):
            mul(1, PACK - 1, c * P, (c + 1) * P, end_ps[c][:, 0:P])

        bf0 = new("bf0", [P, HALF, PACK], BF16)
        for c0, c1, copy in ((0, LOW_SCALAR_COLS, nc.scalar.copy), (LOW_SCALAR_COLS, HALF, nc.vector.tensor_copy)):
            copy(
                out=bf0[:, c0:c1, :].rearrange("p (c e) i -> p c i e", e=4),
                in_=res[0][:, :, c0:c1].rearrange("p i (c e) -> p c i e", e=4),
            )
        mul(1, 0, 0, HALF, y1_ps[0][:])
        mul(1, 1, 0, HALF, y1_ps[1][:])
        store(1, 0, 2)
        o_quant(bf0, 0)
        store_words(0, HALF)
        mul(1, 2, 0, HALF, y1_ps[2][:])
        store(1, 2, 3)
        mul_end(0)
        bf10 = interleave("bf10", res[1], 0, P, nc.scalar.copy)
        mul_end(1)
        bf11 = interleave("bf11", res[1], P, P, nc.scalar.copy)
        mul_end(2)
        o_quant(bf10, HALF)
        mul_end(3)
        store(1, 3, 4)
        bf13 = interleave("bf13", res[1], 3 * P, P, nc.scalar.copy)
        bf12 = interleave("bf12", res[1], 2 * P, P, nc.vector.tensor_copy)
        o_quant(bf11, HALF + P)
        o_quant(bf12, HALF + 2 * P)
        o_quant(bf13, HALF + 3 * P)
        store_words(HALF, M)
        for r in range(4):
            queue = nc.scalar if r % 2 == 0 else nc.sync
            queue.dma_start(
                out=out_2[0].rearrange("(q r) n -> r q n", r=4)[r].bitcast(I32), in_=o_scales[r:P:32, :].bitcast(I32)
            )
